import numpy as np, ml_dtypes
CORES = [242,247,114,119]
N = 4
BF = ml_dtypes.bfloat16
S, M, CAP, L = 768, 512, 256, 5
F = 16 // N
def tries(rng, same=False, few=False):
    kid = np.zeros((N, 8, M, 16), np.int32); words = {}; deep = {}
    tid = (rng.integers(1, 65536, (N, 8, M)) * (rng.random((N, 8, M)) < (0.0625 if few else 0.5))).astype(np.int32)
    for q in range(N):
        for g in range(8):
            no = [0, 1] + (2 + rng.permutation(M - 2)).tolist(); pl = rng.random(M).tolist(); cl = rng.integers(0, 16, M).tolist()
            k = kid[q, g]; w = {1: []}; up = []; m = 2; deep[q, g] = []
            for c in (q * F + rng.permutation(F)).tolist()[:1 if few else F]:
                p = 1
                for d in range(L):
                    e = c if d == 0 or same else cl[m]
                    k[no[p], e] = no[m]; w[m] = w[p] + [e]
                    if d < L - 1: up.append(m)
                    p = m; m += 1
                tid[q, g, no[p]] = rng.integers(1, 65536); deep[q, g].append(w[p])
            for m in range(m, M):
                p = up[int(pl[m] * len(up))]; e = cl[m]
                if k[no[p], e]: continue
                k[no[p], e] = no[m]; w[m] = w[p] + [e]
                if len(w[m]) < L: up.append(m)
            words[q, g] = [v for v in w.values() if v]
    tid[:, :, 0] = 0
    return kid.reshape(N, 8, 16 * M), tid, words, deep
def strings(rng, words):
    s = np.zeros((8, N * S), np.int64)
    for g in range(8):
        qs = rng.integers(0, N, N * S).tolist(); ms = rng.random(N * S).tolist(); a = []; i = 0
        while len(a) < N * S:
            v = words[qs[i], g]; a += v[int(ms[i] * len(v))]; i += 1
        s[g] = a[:N * S]
    return np.where(rng.random(s.shape) < 0.1, rng.integers(0, 16, s.shape), s)
def plant(rng, s, deep):
    keep = np.zeros(s.shape, bool)
    for r in range(N):
        for g in range(8):
            v = deep[int(rng.integers(0, N)), g]; j = (r * S + S - 1 - g % (L - 1) + np.arange(L)) % (N * S)
            s[g, j] = v[int(rng.integers(0, len(v)))]; keep[g, j] = True
    return keep
def fit(rng, s, keep, full=False):
    s = s.reshape(8, N, S).transpose(1, 0, 2).astype(np.int32); keep = keep.reshape(8, N, S).transpose(1, 0, 2)
    a, b = int(rng.integers(0, N)), int(rng.integers(0, 8))
    for r in range(N):
        for g in range(8):
            e = s[r, g]; own = e // F; have = np.bincount(own, minlength=N); low = np.bincount(own[keep[r, g]], minlength=N)
            o = rng.permutation(N); i = np.flatnonzero((o == a) if full and g == b else (o != r))[0]; o[[0, i]] = o[[i, 0]]
            want = low.copy() if full else np.minimum(have, CAP)
            if full or (r, g) == (a, b): want[o[0]] = CAP
            for q in np.roll(o, -1): want[q] = min(max(int(want[q]) + S - int(np.sum(want)), int(low[q])), CAP)
            sur = np.concatenate([rng.permutation(np.flatnonzero((own == q) & ~keep[r, g]))[:max(int(have[q] - want[q]), 0)] for q in range(N)])
            need = np.repeat(np.arange(N), np.maximum(want - have, 0))
            e[sur] = need * F + rng.integers(0, F, len(need))
    return np.ascontiguousarray(s)
def setup_inputs(rng):
    kid, tid, words, deep = tries(rng); s = strings(rng, words); keep = plant(rng, s, deep)
    return {"lett": fit(rng, s, keep), "kid": kid, "tid": tid}
def setup_inputs_full(rng):
    kid, tid, words, deep = tries(rng); s = strings(rng, words)
    lett = fit(rng, s, np.zeros(s.shape, bool), True)
    assert np.sum((lett // F)[..., None] == np.arange(N), axis=2).min(axis=0).max() == CAP
    return {"lett": lett, "kid": kid, "tid": tid}
def setup_inputs_runs(rng):
    kid, tid, words, deep = tries(rng, same=True)
    s = np.stack([np.repeat(rng.integers(0, 16, N * S), rng.integers(1, 13, N * S))[:N * S] for g in range(8)]); keep = plant(rng, s, deep)
    return {"lett": fit(rng, s, keep), "kid": kid, "tid": tid}
def setup_inputs_few(rng):
    kid, tid, words, deep = tries(rng, few=True); s = strings(rng, words); keep = plant(rng, s, deep)
    return {"lett": fit(rng, s, keep), "kid": kid, "tid": tid}
def setup_inputs_spread(rng):
    kid = (rng.integers(0, M, (N, 8, M, 16)) * (rng.random((N, 8, M, 16)) > 0.125)).astype(np.int32)
    kid[:, :, 0] = 0; kid[:, :, 1] *= (np.arange(16) // F == np.arange(N)[:, None])[:, None, :]
    tid = (rng.integers(0, 65536, (N, 8, M)) * (rng.random((N, 8, M)) < 0.3)).astype(np.int32); tid[:, :, 0] = 0; tid[:, :, M - 1] = 65535
    s = np.minimum(np.floor(rng.random((8, N * S)) ** 2 * 16), 15).astype(np.int64)
    return {"lett": fit(rng, s, np.zeros(s.shape, bool)), "kid": kid.reshape(N, 8, 16 * M), "tid": tid}
def check_inputs(d):
    bad = []; s, kid, tid = d["lett"], d["kid"], d["tid"]
    if s.min() < 0 or s.max() > 15: bad.append("letters")
    if ((s // F)[..., None] == np.arange(N)).sum(2).max() > CAP: bad.append("slots")
    if kid.min() < 0 or kid.max() >= M: bad.append("children")
    if kid[:, :, :16].any() or tid[:, :, 0].any(): bad.append("node 0")
    if (kid[:, :, 16:32] * (np.arange(16) // F != np.arange(N)[:, None])[:, None, :]).any(): bad.append("roots")
    if tid.min() < 0 or tid.max() > 65535: bad.append("ids")
    return bad
def reference(lett, kid, tid):
    s = np.concatenate(list(lett), axis=1).astype(np.int64)
    own = s // F; g = np.arange(8)[:, None]; node = np.ones(s.shape, np.int64); yl = np.zeros(s.shape, np.int64); yi = np.zeros(s.shape, np.int64)
    for k in range(L):
        node = kid[own, g, 16 * node + np.roll(s, -k, axis=1)].astype(np.int64)
        t = tid[own, g, node]
        yl = np.where(t > 0, k + 1, yl); yi = np.where(t > 0, t, yi)
    yl = np.ascontiguousarray(yl.reshape(8, N, S).transpose(1, 0, 2)); yi = np.ascontiguousarray(yi.reshape(8, N, S).transpose(1, 0, 2))
    return {"ylen": yl.astype(np.float32), "yid": yi.astype(np.float32)}

@@ -1,0 +1,341 @@
+from concourse.bass import DstId, RemoteDMATransfer
+from concourse.mybir import AluOpType as Op, ActivationFunctionType as Act, AxisListType
+
+S, M = 768, 512
+H = S // 2
+MW = 80
+R = 80
+C = 131072.0
+BIG = 1.5 * 2.0 ** 40
+NONE = -2.0 ** 24
+SCRATCH = {"x": ("sbuf", [128, 4, 8, 16], "int32"), "xb": ("sbuf", [128, 8, 4, 16], "bfloat16")}
+for _t, _s in (("int32", "li52 lh4 ti64 thi64 tlo64 rw1 pi1 ci1 gi1 oi1 lq48 lp48 ln48 lm48 ls48 rowi128 yv64"),
+               ("float32", "tz64 pf1 gf1 cf1 hf1 basec1 rootc1 grp8 best192 rr192 yl192 yi192"),
+               ("uint16", "rown2 rall2 lown4 rl20 letl48 lx52"),
+               ("bfloat16", "sm320 lf4 w2048 v2048 e832 sel2048 y1024 ones192 far32 idb128 sha128 shb128 u16 base48 "
+                            "r320 rid16 ridb320")):
+    for _n in _s.split():
+        _b = _n.rstrip("0123456789")
+        SCRATCH[_b] = ("sbuf", [128, int(_n[len(_b):])], _t)
+for _k in (3, 4, 5):
+    SCRATCH["list%d" % _k] = ("sbuf", [128, 48], "uint16")
+for _k in range(1, 6):
+    SCRATCH["a%d" % _k] = ("sbuf", [128, S], "bfloat16")
+for _k in (2, 3, 4):
+    SCRATCH["m%d" % _k] = ("sbuf", [128, S], "bfloat16")
+for _k in range(8):
+    SCRATCH["pb%d" % _k] = ("psum", [128, 512], "float32")
+SEMAPHORES = ("ld_lett ld_halo ld_tid ld_tid2 ld_root ld_kid0 ld_kid1 ld_kid2 ld_kid3 sm_arr w_arr r_arr sm_out w_out r_out st_id "
+              "st_len iota iota2 z_sel z_sel2 z_y z_ones z_sm z_sh z_rl c_a c_b c_o c_bc c_id c_u c_sh c_grp c_y c_sel s_th "
+              "s_id s_sm l_x l_a l_b l_c l_e l_l l_e2 l_l2 b_base p_halo l_h l_hx o_ls o_l2 w_own r_tmp r_own e_main e_halo r_col "
+              "r_all r_l a_rid a_ridb a_id1 a_id2 a_id3 x_conv0 x_conv1 p_x0 p_x1 p_x2 p_x3 p_v0 p_v1 p_v2 p_v3 v_in v_in2 "
+              "p_z1 p_z2 p_z3 p_z4 d1 d2 d3 d4 a_id5").split()
+for _f in "ab":
+    SEMAPHORES += [_n + _f for _n in ("v_m2", "v_m3", "v_m4", "p_list3", "p_list4", "p_list5", "v_list3", "v_list4", "v_list5",
+                                      "a_id4", "v_id5", "p_z5", "d5", "rr_ok", "yi_ok", "yl_ok")]
+
+
+def rank_program(g, core, T, topo):
+    rank = T.rank_of(core)
+    if rank is None:
+        return
+    n = len(T.cores)
+    v, pe, act, sp = g.vector, g.tensor, g.scalar, g.sync
+    count = {}
+
+    def inc(call, name, by=1):
+        call.then_inc(T.sem[name], by)
+        count[name] = count.get(name, 0) + by
+
+    def need(queue, *names):
+        for name in names:
+            queue.wait_ge(T.sem[name], count[name])
+
+    def ts(name, out, in0, s1, op0, s2=None, op1=None):
+        inc(v.tensor_scalar(out, in0, s1, None, op0) if op1 is None else v.tensor_scalar(out, in0, s1, s2, op0, op1), name)
+
+    near = [d for d in T.cores if d != core and d in topo.cores_of(core)]
+    far = [d for d in T.cores if d != core and d not in topo.cores_of(core)]
+    far_e = [e for e in range(16) if all(e in topo.engines(core, d) for d in far)]
+    near_e = [e for e in range(16) if all(e in topo.engines(core, d) for d in near) and e not in far_e]
+    near_e = near_e[:len(far_e) * len(near) // len(far)]
+
+    def spread(src, dst, arr, out):
+        tr = []
+        for ds, es in ((far, far_e), (near, near_e)):
+            ids = []
+            for d in ds:
+                rid, pid = topo.addr(d, core)
+                ids.append(DstId(rid=rid, pnc=pid))
+            tr.append(RemoteDMATransfer(dst_ids=ids, dma_engine_mask=sum(1 << e for e in es),
+                                        remote_sem=T.sem[arr], srcs=[src], dsts=[dst for _ in ds]))
+            count[out] = count.get(out, 0) + len(es)
+            count[arr] = count.get(arr, 0) + len(es) * len(ds)
+        g.remote_dma_fused(tr, local_sem=T.sem[out])
+
+    c0, cw, r0, o = MW * rank, M * rank, R * rank, 4 * rank
+    lo64, hi64 = slice(0, 64), slice(64, 128)
+    inc(act.dma_start(T.rw[:, 0:1], T.kid[:, 16:32]), "ld_root", 16)
+    inc(sp.dma_start(T.ti[lo64, :], T.tid[:, :]), "ld_tid", 16)
+    inc(sp.dma_start(T.lh[0:8, :], T.lett[:, 0:4]), "ld_halo", 16)
+    inc(act.dma_start(T.ti[hi64, :], T.tid[:, :]), "ld_tid2", 16)
+    for q4 in range(4):
+        inc((act, sp)[q4 % 2].dma_start(T.x[:, q4, :, :], T.kid[q4:8:4, :]), "ld_kid%d" % q4, 16)
+    inc(sp.dma_start(T.li[:, 0:48], T.lett[:, :]), "ld_lett", 16)
+
+    inc(g.iota(T.pi[:, :], [[0, 1]], 0, 1), "iota")
+    inc(g.iota(T.rowi[:, :], [[1, 128]], 0, 0), "iota")
+    inc(g.iota(T.yv[:, :], [[1, 8], [8, 8]], 0, 0), "iota2")
+    inc(v.memset(T.sm[:, c0:c0 + 16], 0.0), "z_sm")
+    inc(v.memset(T.sel[:, 0:1024], 0.0), "z_sel")
+    need(v, "iota")
+    ts("c_a", T.ci[:, :], T.pi[:, :], 15, Op.bitwise_and)
+    ts("c_a", T.gi[:, :], T.pi[:, :], 4, Op.arith_shift_right)
+    inc(v.tensor_copy(T.pf[:, :], T.pi[:, :]), "c_a")
+    inc(v.memset(T.ones[:, :], 1.0), "z_ones")
+    inc(v.memset(T.far[:, :], C), "z_ones")
+    need(v, "c_a")
+    ts("c_id", T.idb[:, :], T.rowi[:, :], T.pf[:, :], Op.is_equal)
+    inc(v.tensor_copy(T.cf[:, :], T.ci[:, :]), "c_b")
+    inc(v.tensor_copy(T.gf[:, :], T.gi[:, :]), "c_b")
+    ts("c_b", T.hf[:, :], T.pf[:, :], 16.0, Op.mult, 15.0, Op.add)
+    ts("c_o", T.oi[:, :], T.ci[:, :], 2, Op.arith_shift_right)
+    need(act, "z_sel")
+    inc(act.activation(T.y[:, :], T.sel[:, 0:1024], Act.Copy), "z_y")
+    inc(act.activation(T.sel[:, 1024:2048], T.sel[:, 0:1024], Act.Copy), "z_sel2")
+
+    need(v, "ld_tid")
+    ts("s_th", T.thi[lo64, :], T.ti[lo64, :], 65280, Op.bitwise_and)
+    ts("s_th", T.tz[lo64, :], T.ti[lo64, :], 0.0, Op.is_equal, NONE, Op.mult)
+    need(v, "ld_tid2")
+    ts("s_th", T.tlo[hi64, :], T.ti[hi64, :], 255, Op.bitwise_and)
+    need(v, "ld_root", "z_sm")
+    ts("s_sm", T.sm[:, c0:c0 + 1], T.rw[:, 0:1], -256.0, Op.add)
+    need(v, "s_th")
+    inc(v.tensor_tensor(T.sm[lo64, c0 + 16:c0 + 80], T.thi[lo64, :], T.tz[lo64, :], Op.add), "s_id")
+    inc(v.tensor_copy(T.sm[hi64, c0 + 16:c0 + 80], T.tlo[hi64, :]), "s_id")
+    need(v, "ld_halo")
+    inc(v.tensor_copy(T.sm[0:8, c0 + 8:c0 + 12], T.lh[0:8, :]), "s_sm")
+    need(g, "s_sm", "s_id")
+    spread(T.sm[:, c0:c0 + MW], T.sm[:, c0:c0 + MW], "sm_arr", "sm_out")
+    inc(v.tensor_copy(T.rown[:, 0:1], T.rw[:, 0:1]), "o_ls")
+    need(v, "c_b", "c_o")
+    ts("c_u", T.u[:, :], T.rowi[:, 0:16], T.cf[:, :], Op.is_equal)
+    ts("c_grp", T.grp[:, :], T.rowi[:, 0:8], T.gf[:, :], Op.is_equal)
+    ts("c_sh", T.shb[:, :], T.rowi[:, :], T.hf[:, :], Op.is_equal)
+    need(v, "iota2", "z_y", "c_id")
+    ts("c_y", T.y[:, 0:1024:16], T.yv[:, :], T.pf[:, :], Op.is_equal)
+    ts("c_y", T.y[:, 1:1024:16], T.yv[:, :], 64.0, Op.add, T.pf[:, :], Op.is_equal)
+
+    for q4 in range(4):
+        need(v, "ld_kid%d" % q4)
+        for par in range(2):
+            ts("x_conv%d" % par, T.xb[:, par:8:2, q4, :], T.x[:, q4, par:8:2, :], -256.0, Op.add)
+    xbank = [T.pb2, T.pb3, T.pb4, T.pb6]
+    need(pe, "c_id")
+    for u in (0, 2, 1, 3):
+        need(pe, "x_conv%d" % (u % 2))
+        for j in range(2):
+            for a in range(2):
+                p = slice(64 * a, 64 * a + 64)
+                inc(pe.matmul(xbank[u][p, j:128:2], T.xb[p, u + 4 * j, :, :], T.idb[p, p], True, True), "p_x%d" % u)
+    for u in (0, 2, 1, 3):
+        queue = (act, v)[u % 2]
+        need(queue, "p_x%d" % u)
+        land, bank = T.w[:, cw + u:cw + M:4], xbank[u][:, 0:128]
+        inc(act.activation(land, bank, Act.Copy) if u % 2 == 0 else v.tensor_copy(land, bank), "w_own")
+    need(v, "w_own", "o_ls")
+    inc(v.tensor_copy(T.r[:, r0 + 64:r0 + 80], T.w[:, cw:cw + M].indirect(T.rown[:, 0:1])), "r_tmp")
+    need(v, "r_tmp")
+    ts("o_l2", T.lown[:, 0:4], T.r[:, r0 + 64 + o:r0 + 68 + o], 256.0, Op.add)
+    need(v, "o_l2")
+    inc(v.tensor_copy(T.r[:, r0:r0 + 64], T.w[:, cw:cw + M].indirect(T.lown[:, 0:4])), "r_own")
+    need(g, "r_tmp", "r_own")
+    spread(T.r[:, r0:r0 + R], T.r[:, r0:r0 + R], "r_arr", "r_out")
+    need(g, "w_own")
+    spread(T.w[:, cw:cw + M], T.w[:, cw:cw + M], "w_arr", "w_out")
+
+    need(v, "ld_lett")
+    inc(v.tensor_copy(T.lx[:, 0:48], T.li[:, 0:48]), "l_x")
+    need(act, "l_x", "c_u")
+    inc(act.activation(T.e[:, 32:S], T.u[:, 0:16].indirect(T.lx[:, 2:48]), Act.Copy), "e_main")
+    ts("l_a", T.lq[:, :], T.li[:, 0:48], 12, Op.bitwise_and)
+    ts("l_a", T.ln[:, :], T.li[:, 0:48], 16.0, Op.mult)
+    inc(v.tensor_copy(T.sha[:, 0:127], T.idb[:, 1:128]), "z_sh")
+    need(v, "l_a")
+    ts("l_b", T.lp[:, :], T.lq[:, :], 4.0, Op.mult)
+    ts("b_base", T.base[:, :], T.lq[:, :], 128.0, Op.mult, 256.0, Op.add)
+    need(v, "z_sh")
+    inc(v.memset(T.sha[:, 15:128:16], 0.0), "c_sh")
+    need(v, "l_b")
+    inc(v.tensor_tensor(T.lm[:, :], T.ln[:, :], T.lp[:, :], Op.add), "l_c")
+    inc(v.tensor_copy(T.lf[:, :], T.li[:, 0:4]), "l_h")
+    need(v, "l_c")
+    inc(v.tensor_tensor(T.ls[:, 0:24], T.lm[:, 0:24], T.li[:, 1:25], Op.add), "l_e")
+    inc(v.memset(T.rl[:, :], 0), "z_rl")
+    need(v, "l_e")
+    inc(v.tensor_copy(T.letl[:, 0:24], T.ls[:, 0:24]), "l_l")
+    need(v, "c_grp", "z_sel", "z_sel2", "z_ones")
+    for h in range(8):
+        ts("c_sel", T.sel[:, 16 * h:2048:129], T.ones[:, 0:16], T.grp[:, h:h + 1], Op.mult)
+    ts("c_bc", T.basec[:, :], T.oi[:, :], 512.0, Op.mult, 1024.0, Op.add)
+
+    cn = MW * ((rank + 1) % n)
+    vb = [T.pb0, T.pb1, T.pb5, T.pb7]
+    need(pe, "c_y", "s_id")
+    for j in range(n):
+        q = (rank + j) % n
+        if j == 1:
+            need(pe, "c_sh", "l_h", "w_own", "s_sm", "sm_arr")
+            pe.matmul(T.pb2[:, 0:4], T.sha[:, :], T.lf[:, :], True, False)
+            inc(pe.matmul(T.pb2[:, 0:4], T.shb[0:8, :], T.sm[0:8, cn + 8:cn + 12], False, True), "p_halo")
+        for b in range(8):
+            inc(pe.matmul(vb[j][:, 64 * b:64 * b + 64], T.y[:, 128 * b:128 * b + 128], T.sm[:, MW * q + 16:MW * q + 80],
+                          True, True), "p_v%d" % j)
+        if j < n - 1:
+            need(act, "p_v%d" % j)
+            inc(act.activation(T.v[:, M * q:M * q + M], vb[j][:, :], Act.Copy), "v_in")
+    need(v, "p_halo")
+    inc(v.tensor_copy(T.li[:, 48:52], T.pb2[:, 0:4]), "l_hx")
+    inc(v.tensor_copy(T.lx[:, 48:52], T.pb2[:, 0:4]), "l_hx")
+    need(v, "sm_arr", "s_sm")
+    inc(v.tensor_reduce(T.rootc[:, :], T.sm[:, 0:MW * n:MW], AxisListType.X, Op.add), "r_col")
+    need(v, "l_hx", "c_u")
+    inc(v.tensor_tensor(T.ls[:, 24:48], T.lm[:, 24:48], T.li[:, 25:49], Op.add), "l_e2")
+    inc(v.tensor_copy(T.e[:, S:S + 64], T.u[:, 0:16].indirect(T.lx[:, 48:52])), "e_halo")
+    need(v, "l_e2")
+    inc(v.tensor_copy(T.letl[:, 24:48], T.ls[:, 24:48]), "l_l2")
+    need(v, "r_col", "c_bc")
+    ts("r_all", T.rall[:, 0:1], T.rootc[:, :], T.basec[:, :], Op.add)
+    need(v, "p_v%d" % (n - 1))
+    inc(v.tensor_copy(T.v[:, M * q:M * q + M], vb[n - 1][:, :]), "v_in2")
+
+    win, win2 = T.w[:, 0:4 * M], T.v[:, 0:4 * M]
+    lbank = {"a": T.pb2, "b": T.pb3}
+    zb = {1: T.pb0, 2: T.pb1, 3: T.pb5, 4: T.pb7}
+    z5 = {"a": T.pb4, "b": T.pb6}
+    part = {"a": 0, "b": 1}
+
+    def step(k, f):
+        h = part[f]
+        src = T.r[:, 0:4 * R].indirect(T.letl[:, 24 * h:24 * h + 24]) if k == 2 else \
+            win.indirect(T["list%d" % k][:, 24 * h:24 * h + 24])
+        inc(v.tensor_tensor(T["m%d" % k][:, H * h:H * h + H], src, T.e[:, 16 * k + H * h:16 * k + H * h + H], Op.mult),
+            "v_m%d%s" % (k, f))
+
+    def wrap(k, f):
+        h = part[f]
+        if k > 2:
+            need(pe, "v_list%d%s" % (k, f))
+        out = lbank[f][:, 0:24]
+        pe.matmul(out, T.idb[:, :], T.base[:, 24 * h:24 * h + 24], True, False)
+        need(pe, "v_m%d%s" % (k, f))
+        for i in range(16):
+            call = pe.matmul(out, T.sel[:, 128 * i:128 * i + 128], T["m%d" % k][:, H * h + i:H * h + H:16], False, i == 15)
+        inc(call, "p_list%d%s" % (k + 1, f))
+
+    def take(k, f):
+        h = part[f]
+        need(v, "p_list%d%s" % (k, f))
+        inc(v.tensor_copy(T["list%d" % k][:, 24 * h:24 * h + 24], lbank[f][:, 0:24]), "v_list%d%s" % (k, f))
+        need(v, "v_list%d%s" % (k, f))
+
+    def add_far(k, z):
+        pe.matmul(z, T.far[0:k, :], T.ones[0:k, 0:z.shape[1]], True, False)
+
+    def sums(k, z, col, s, last):
+        for b in range(4):
+            i = 4 * b + s
+            call = pe.matmul(z[0:32, col:col + 48], T.sel[:, 128 * i + s:128 * i + 128:4], T["a%d" % k][:, i:S:16],
+                             False, last and b == 3)
+        return call
+
+    def ids(k, *waits):
+        need(pe, *waits)
+        for s in range(4):
+            call = sums(k, zb[k], 48 * s, s, s == 3)
+        inc(call, "p_z%d" % k)
+
+    def keep(k):
+        need(v, "p_z%d" % k, "d%d" % (k - 1))
+        inc(v.tensor_tensor(T.best[0:32, :], zb[k][0:32, 0:192], T.best[0:32, :], Op.max), "d%d" % k)
+
+    need(act, "v_in", "v_in2", "r_all")
+    inc(act.activation(T.rid[:, :], win2.indirect(T.rall[:, 0:1]), Act.Copy), "a_rid")
+    need(act, "a_rid")
+    inc(act.activation(T.a1[:, :], T.rid[:, 0:16].indirect(T.lx[:, 0:48]), Act.Copy), "a_id1")
+    need(v, "r_arr", "l_l", "e_main")
+    step(2, "a")
+    need(v, "l_l2", "e_halo")
+    step(2, "b")
+    need(v, "z_rl")
+    for q in range(n):
+        ts("r_l", T.rl[:, 5 * q:5 * q + 4], T.r[:, R * q + 64 + 4 * q:R * q + 68 + 4 * q], 256.0 + M * q, Op.add)
+    need(act, "r_l")
+    inc(act.activation(T.ridb[:, :], win2.indirect(T.rl[:, 0:20]), Act.Copy), "a_ridb")
+    need(act, "a_ridb", "l_l", "l_l2")
+    inc(act.activation(T.a2[:, :], T.ridb[:, 0:4 * R].indirect(T.letl[:, 0:48]), Act.Copy), "a_id2")
+    need(pe, "b_base", "c_sel", "l_hx", "z_ones")
+    for f in "ab":
+        add_far(5, z5[f][0:32, 0:96])
+    wrap(2, "a")
+    wrap(2, "b")
+    need(pe, "v_in", "v_in2")
+    for k in (1, 2, 3, 4):
+        add_far(k, zb[k][0:32, 0:192])
+    ids(1, "a_id1")
+    take(3, "a")
+    take(3, "b")
+    need(act, "v_list3a", "v_list3b")
+    inc(act.activation(T.a3[:, :], win2.indirect(T.list3[:, 0:48]), Act.Copy), "a_id3")
+    need(v, "w_arr")
+    step(3, "a")
+    step(3, "b")
+    wrap(3, "a")
+    wrap(3, "b")
+    ids(2, "a_id2")
+    for f in "ab":
+        take(4, f)
+        step(4, f)
+        h = part[f]
+        need(act, "v_list4" + f)
+        inc(act.activation(T.a4[:, H * h:H * h + H], win2.indirect(T.list4[:, 24 * h:24 * h + 24]), Act.Copy), "a_id4" + f)
+        wrap(4, f)
+    ids(3, "a_id3")
+    ids(4, "a_id4a", "a_id4b")
+    need(act, "p_z1")
+    inc(act.activation(T.best[0:32, :], zb[1][0:32, 0:192], Act.Relu), "d1")
+    need(v, "v_in", "v_in2")
+    take(5, "a")
+    inc(v.tensor_copy(T.a5[:, 0:H], win2.indirect(T.list5[:, 0:24])), "v_id5a")
+    take(5, "b")
+    inc(v.tensor_copy(T.a5[:, H:H + 192], win2.indirect(T.list5[:, 24:36])), "v_id5b")
+    need(act, "v_list5b")
+    inc(act.activation(T.a5[:, H + 192:S], win2.indirect(T.list5[:, 36:48]), Act.Copy), "a_id5")
+    for k in (2, 3, 4):
+        keep(k)
+    need(pe, "v_id5a", "v_id5b", "a_id5")
+    for f in "ab":
+        for j in range(2):
+            call = sums(5, z5[f], 48 * j, 2 * part[f] + j, j == 1)
+        inc(call, "p_z5" + f)
+
+    half = {f: slice(96 * part[f], 96 * part[f] + 96) for f in "ab"}
+    for f in "ab":
+        need(v, "p_z5" + f, "d4")
+        inc(v.tensor_tensor(T.pb2[0:32, half[f]], z5[f][0:32, 0:96], T.best[0:32, half[f]], Op.max), "d5" + f)
+    for f in "ab":
+        need(v, "d5" + f)
+        ts("rr_ok" + f, T.rr[0:32, half[f]], T.pb2[0:32, half[f]], BIG, Op.add, -BIG, Op.add)
+    for f in "ab":
+        need(v, "rr_ok" + f)
+        inc(v.tensor_tensor(T.yi[0:32, half[f]], T.pb2[0:32, half[f]], T.rr[0:32, half[f]], Op.subtract), "yi_ok" + f)
+        need(act, "rr_ok" + f)
+        inc(act.activation(T.yl[0:32, half[f]], T.rr[0:32, half[f]], Act.Copy, scale=1.0 / C), "yl_ok" + f)
+    need(act, "yl_oka", "yl_okb")
+    inc(act.dma_start(T.ylen[:, :], T.yl[0:32, :]), "st_len", 16)
+    need(sp, "yi_oka", "yi_okb")
+    inc(sp.dma_start(T.yid[:, :], T.yi[0:32, :]), "st_id", 16)
+    need(act, "st_len")
+    need(sp, "st_id")
+    need(g, "sm_out", "w_out", "r_out")

@@ -1,38 +1,42 @@
 from concourse.bass import DstId, RemoteDMATransfer
-from concourse.mybir import AluOpType as Op, ActivationFunctionType as Act, AxisListType
+from concourse.mybir import AluOpType as Op, ActivationFunctionType as Act
 
 S, M = 768, 512
 H = S // 2
-MW = 80
-R = 80
+MW = 72
+R = 64
 C = 131072.0
 BIG = 1.5 * 2.0 ** 40
 NONE = -2.0 ** 24
+OPT = dict(i12="3a", i3="3b", i4=True, end="La na Lb ra nb rb", order="fn on", fe="all", l8=False, a5="act")
 SCRATCH = {"x": ("sbuf", [128, 4, 8, 16], "int32"), "xb": ("sbuf", [128, 8, 4, 16], "bfloat16")}
-for _t, _s in (("int32", "li52 lh4 ti64 thi64 tlo64 rw1 pi1 ci1 gi1 oi1 lq48 lp48 ln48 lm48 ls48 rowi128 yv64"),
-               ("float32", "tz64 pf1 gf1 cf1 hf1 basec1 rootc1 grp8 best192 rr192 yl192 yi192"),
-               ("uint16", "rown2 rall2 lown4 rl20 letl48 lx52"),
-               ("bfloat16", "sm320 lf4 w2048 v2048 e832 sel2048 y1024 ones192 far32 idb128 sha128 shb128 u16 base48 "
-                            "r320 rid16 ridb320")):
+for _t, _s in (("int32", "li52 hm4 hin4 rw1 ti64 tb64 pi1 ci1 gi1 pq1 lq48 ln48 ls48 rowi144 yv64"),
+               ("float32", "tz64 pf1 cf1 hf1 hq1 hs1 hz1 cap1 wk4 wb1 first4 ma64 mt64"),
+               ("uint16", "rown2 rtwin2 lown16 ltwin16 ld48 lx52"),
+               ("bfloat16", "mul1 cu1 lf4 hb4 sm288 w2048 v2048 e832 sel144 y1024 idb128 sha128 shb128 shr128 u16 base48 r256 "
+                            "d256 rid16 gb64")):
     for _n in _s.split():
         _b = _n.rstrip("0123456789")
         SCRATCH[_b] = ("sbuf", [128, int(_n[len(_b):])], _t)
+for _n in ("best", "rr", "yl", "yi"):
+    SCRATCH[_n] = ("sbuf", [128, 4, 48], "float32")
 for _k in (3, 4, 5):
     SCRATCH["list%d" % _k] = ("sbuf", [128, 48], "uint16")
-for _k in range(1, 6):
+for _k in range(2, 6):
     SCRATCH["a%d" % _k] = ("sbuf", [128, S], "bfloat16")
+    SCRATCH["z%d" % _k] = ("sbuf", [128, 144], "bfloat16")
 for _k in (2, 3, 4):
     SCRATCH["m%d" % _k] = ("sbuf", [128, S], "bfloat16")
 for _k in range(8):
     SCRATCH["pb%d" % _k] = ("psum", [128, 512], "float32")
-SEMAPHORES = ("ld_lett ld_halo ld_tid ld_tid2 ld_root ld_kid0 ld_kid1 ld_kid2 ld_kid3 sm_arr w_arr r_arr sm_out w_out r_out st_id "
-              "st_len iota iota2 z_sel z_sel2 z_y z_ones z_sm z_sh z_rl c_a c_b c_o c_bc c_id c_u c_sh c_grp c_y c_sel s_th "
-              "s_id s_sm l_x l_a l_b l_c l_e l_l l_e2 l_l2 b_base p_halo l_h l_hx o_ls o_l2 w_own r_tmp r_own e_main e_halo r_col "
-              "r_all r_l a_rid a_ridb a_id1 a_id2 a_id3 x_conv0 x_conv1 p_x0 p_x1 p_x2 p_x3 p_v0 p_v1 p_v2 p_v3 v_in v_in2 "
-              "p_z1 p_z2 p_z3 p_z4 d1 d2 d3 d4 a_id5").split()
+SEMAPHORES = ("ld_lett ld_halo ld_root ld_tid ld_tid2 ld_kid0 ld_kid1 ld_kid2 ld_kid3 ld_kid4 ld_kid5 ld_kid6 ld_kid7 h_arr sm_arr "
+              "w_twin w_near w_on r_arr d_near d_far sent st_id st_len iota iota2 z_y z_hm z_sm z_sh c_a c_b c_id c_u c_h c_h0 "
+              "c_hs c_shr c_sh c_hz c_y c_sel c_w c_wk c_wb c_z s_th s_id s_sm l_x l_a l_s l_d b_base p_halo p_ro p_rt l_h l_hb "
+              "l_hx o_ls o_l2 w_own r_own t_ls t_l2 t_own e_main e_halo a_rid a_gb g_c g_m d_own a_id2 a_id3 x_lo x_conv0 x_conv1 "
+              "p_x0 p_x1 p_x2 p_x3 p_v0 p_v1 p_v2 p_v3 v_own v_in p_z2 p_z3 d2 d3 a_id5").split()
 for _f in "ab":
     SEMAPHORES += [_n + _f for _n in ("v_m2", "v_m3", "v_m4", "p_list3", "p_list4", "p_list5", "v_list3", "v_list4", "v_list5",
-                                      "a_id4", "v_id5", "p_z5", "d5", "rr_ok", "yi_ok", "yl_ok")]
+                                      "a_id4", "p_z4", "d4", "v_id5", "p_z5", "d5", "rr_ok", "yi_ok", "yl_ok")]
 
 
 def rank_program(g, core, T, topo):
@@ -56,169 +60,233 @@ def rank_program(g, core, T, topo):
 
     near = [d for d in T.cores if d != core and d in topo.cores_of(core)]
     far = [d for d in T.cores if d != core and d not in topo.cores_of(core)]
+    twin = [d for d in far if topo.die(d) == topo.die(core)]
+    other = [d for d in far if d not in twin]
     far_e = [e for e in range(16) if all(e in topo.engines(core, d) for d in far)]
-    near_e = [e for e in range(16) if all(e in topo.engines(core, d) for d in near) and e not in far_e]
-    near_e = near_e[:len(far_e) * len(near) // len(far)]
+    all_e = [e for e in range(16) if all(e in topo.engines(core, d) for d in near)]
+    near_e = [e for e in all_e if e not in far_e]
+    qt, qn, qo = (T.rank_of(d[0]) for d in (twin, near, other))
+    before, after = T.cores[(rank - 1) % n], T.cores[(rank + 1) % n]
 
-    def spread(src, dst, arr, out):
+    def send(piece, land, *ways):
         tr = []
-        for ds, es in ((far, far_e), (near, near_e)):
+        for ds, es, arr in ways:
             ids = []
             for d in ds:
                 rid, pid = topo.addr(d, core)
                 ids.append(DstId(rid=rid, pnc=pid))
             tr.append(RemoteDMATransfer(dst_ids=ids, dma_engine_mask=sum(1 << e for e in es),
-                                        remote_sem=T.sem[arr], srcs=[src], dsts=[dst for _ in ds]))
-            count[out] = count.get(out, 0) + len(es)
+                                        remote_sem=T.sem[arr], srcs=[piece], dsts=[land for _ in ds]))
+            count["sent"] = count.get("sent", 0) + len(es)
             count[arr] = count.get(arr, 0) + len(es) * len(ds)
-        g.remote_dma_fused(tr, local_sem=T.sem[out])
+        g.remote_dma_fused(tr, local_sem=T.sem["sent"])
 
     c0, cw, r0, o = MW * rank, M * rank, R * rank, 4 * rank
     lo64, hi64 = slice(0, 64), slice(64, 128)
-    inc(act.dma_start(T.rw[:, 0:1], T.kid[:, 16:32]), "ld_root", 16)
-    inc(sp.dma_start(T.ti[lo64, :], T.tid[:, :]), "ld_tid", 16)
-    inc(sp.dma_start(T.lh[0:8, :], T.lett[:, 0:4]), "ld_halo", 16)
-    inc(act.dma_start(T.ti[hi64, :], T.tid[:, :]), "ld_tid2", 16)
-    for q4 in range(4):
-        inc((act, sp)[q4 % 2].dma_start(T.x[:, q4, :, :], T.kid[q4:8:4, :]), "ld_kid%d" % q4, 16)
+    inc(sp.dma_start(T.hm[0:32, :], T.lett[:, 0:16]), "ld_halo", 16)
+    inc(act.dma_start(T.ti[lo64, :], T.tid[:, :]), "ld_tid", 16)
+    inc(sp.dma_start(T.ti[hi64, :], T.tid[:, :]), "ld_tid2", 16)
+    inc(act.dma_start(T.rw[0:32, :], T.kid[:, 16 + o:20 + o]), "ld_root", 16)
+    if OPT["l8"]:
+        for h in range(8):
+            inc((sp, act)[h % 2].dma_start(T.x[(lo64, hi64)[h // 4], h % 4, :, :], T.kid[h:h + 1, :]), "ld_kid%d" % h, 16)
+    else:
+        for q4 in range(4):
+            inc((sp, act)[q4 % 2].dma_start(T.x[:, q4, :, :], T.kid[q4:8:4, :]), "ld_kid%d" % q4, 16)
     inc(sp.dma_start(T.li[:, 0:48], T.lett[:, :]), "ld_lett", 16)
 
+    inc(v.memset(T.hm[32:64, :], 0), "z_hm")
+    inc(v.memset(T.hm[hi64, :], 0), "z_hm")
     inc(g.iota(T.pi[:, :], [[0, 1]], 0, 1), "iota")
-    inc(g.iota(T.rowi[:, :], [[1, 128]], 0, 0), "iota")
+    inc(g.iota(T.rowi[:, :], [[1, 144]], 0, 0), "iota")
     inc(g.iota(T.yv[:, :], [[1, 8], [8, 8]], 0, 0), "iota2")
-    inc(v.memset(T.sm[:, c0:c0 + 16], 0.0), "z_sm")
-    inc(v.memset(T.sel[:, 0:1024], 0.0), "z_sel")
+    need(g, "z_hm", "ld_halo")
+    send(T.hm[:, :], T.hin[:, :], ([before], topo.engines(core, before), "h_arr"))
+    count["h_arr"] = len(topo.engines(after, core))
+
+    inc(v.memset(T.sm[:, c0 + 64:c0 + MW], 0.0), "z_sm")
+    inc(v.memset(T.y[:, :], 0.0), "z_y")
     need(v, "iota")
     ts("c_a", T.ci[:, :], T.pi[:, :], 15, Op.bitwise_and)
-    ts("c_a", T.gi[:, :], T.pi[:, :], 4, Op.arith_shift_right)
     inc(v.tensor_copy(T.pf[:, :], T.pi[:, :]), "c_a")
-    inc(v.memset(T.ones[:, :], 1.0), "z_ones")
-    inc(v.memset(T.far[:, :], C), "z_ones")
+    ts("c_h0", T.pq[:, :], T.pi[:, :], 3, Op.bitwise_and)
+    ts("c_h0", T.hq[:, :], T.pi[:, :], 4.0, Op.mult, 15.0, Op.add)
+    ts("c_h0", T.gi[:, :], T.pi[:, :], 4, Op.arith_shift_right)
     need(v, "c_a")
-    ts("c_id", T.idb[:, :], T.rowi[:, :], T.pf[:, :], Op.is_equal)
+    ts("c_id", T.idb[:, :], T.rowi[:, 0:128], T.pf[:, :], Op.is_equal)
     inc(v.tensor_copy(T.cf[:, :], T.ci[:, :]), "c_b")
-    inc(v.tensor_copy(T.gf[:, :], T.gi[:, :]), "c_b")
-    ts("c_b", T.hf[:, :], T.pf[:, :], 16.0, Op.mult, 15.0, Op.add)
-    ts("c_o", T.oi[:, :], T.ci[:, :], 2, Op.arith_shift_right)
-    need(act, "z_sel")
-    inc(act.activation(T.y[:, :], T.sel[:, 0:1024], Act.Copy), "z_y")
-    inc(act.activation(T.sel[:, 1024:2048], T.sel[:, 0:1024], Act.Copy), "z_sel2")
+    ts("c_b", T.mul[:, :], T.ci[:, :], 2.0, Op.is_lt)
+    need(v, "iota2", "z_y")
+    ts("c_y", T.y[:, 0:1024:16], T.yv[:, :], T.pf[:, :], Op.is_equal)
+    for row in (1, 2):
+        ts("c_y", T.y[:, row:1024:16], T.yv[:, :], 64.0, Op.add, T.pf[:, :], Op.is_equal)
+    need(v, "c_b", "c_h0")
+    ts("c_u", T.u[:, :], T.rowi[:, 0:16], T.cf[:, :], Op.is_equal)
+    ts("c_hs", T.hs[:, :], T.pq[:, :], -3.0, Op.mult, T.hq[:, :], Op.add)
 
     need(v, "ld_tid")
-    ts("s_th", T.thi[lo64, :], T.ti[lo64, :], 65280, Op.bitwise_and)
-    ts("s_th", T.tz[lo64, :], T.ti[lo64, :], 0.0, Op.is_equal, NONE, Op.mult)
+    ts("s_th", T.tb[lo64, :], T.ti[lo64, :], 65280, Op.bitwise_and)
     need(v, "ld_tid2")
-    ts("s_th", T.tlo[hi64, :], T.ti[hi64, :], 255, Op.bitwise_and)
-    need(v, "ld_root", "z_sm")
-    ts("s_sm", T.sm[:, c0:c0 + 1], T.rw[:, 0:1], -256.0, Op.add)
+    ts("s_th", T.tb[hi64, :], T.ti[hi64, :], 255, Op.bitwise_and)
+    ts("s_th", T.tz[:, :], T.ti[:, :], 0.0, Op.is_equal, NONE, Op.mult)
+    need(v, "ld_root", "z_sm", "c_hs")
+    ts("s_sm", T.sm[0:32, c0 + 64:c0 + 65], T.rw[0:32, :], -256.0, Op.add)
+    ts("c_shr", T.shr[0:32, :], T.rowi[0:32, 0:128], 15.0, Op.add, T.hs[0:32, :], Op.is_equal)
     need(v, "s_th")
-    inc(v.tensor_tensor(T.sm[lo64, c0 + 16:c0 + 80], T.thi[lo64, :], T.tz[lo64, :], Op.add), "s_id")
-    inc(v.tensor_copy(T.sm[hi64, c0 + 16:c0 + 80], T.tlo[hi64, :]), "s_id")
-    need(v, "ld_halo")
-    inc(v.tensor_copy(T.sm[0:8, c0 + 8:c0 + 12], T.lh[0:8, :]), "s_sm")
-    need(g, "s_sm", "s_id")
-    spread(T.sm[:, c0:c0 + MW], T.sm[:, c0:c0 + MW], "sm_arr", "sm_out")
-    inc(v.tensor_copy(T.rown[:, 0:1], T.rw[:, 0:1]), "o_ls")
-    need(v, "c_b", "c_o")
-    ts("c_u", T.u[:, :], T.rowi[:, 0:16], T.cf[:, :], Op.is_equal)
-    ts("c_grp", T.grp[:, :], T.rowi[:, 0:8], T.gf[:, :], Op.is_equal)
-    ts("c_sh", T.shb[:, :], T.rowi[:, :], T.hf[:, :], Op.is_equal)
-    need(v, "iota2", "z_y", "c_id")
-    ts("c_y", T.y[:, 0:1024:16], T.yv[:, :], T.pf[:, :], Op.is_equal)
-    ts("c_y", T.y[:, 1:1024:16], T.yv[:, :], 64.0, Op.add, T.pf[:, :], Op.is_equal)
+    inc(v.tensor_tensor(T.sm[:, c0:c0 + 64], T.tb[:, :], T.tz[:, :], Op.add), "s_id")
+    need(g, "s_id", "s_sm")
+    send(T.sm[:, c0:c0 + MW], T.sm[:, c0:c0 + MW], (far, far_e, "sm_arr"), (near, near_e, "sm_arr"))
 
-    for q4 in range(4):
-        need(v, "ld_kid%d" % q4)
-        for par in range(2):
-            ts("x_conv%d" % par, T.xb[:, par:8:2, q4, :], T.x[:, q4, par:8:2, :], -256.0, Op.add)
+    vb = {rank: T.pb0, qt: T.pb1, qn: T.pb5, qo: T.pb7}
+
+    def turn_ids(q, done):
+        for b in range(8):
+            call = pe.matmul(vb[q][:, 64 * b:64 * b + 64], T.y[:, 128 * b:128 * b + 128], T.sm[:, MW * q:MW * q + 64], True, True)
+        inc(call, "p_v%d" % q)
+        need(act, "p_v%d" % q)
+        inc(act.activation(T.v[:, M * q:M * q + M], vb[q][:, :], Act.Identity, bias=T.u[:, 3:4]), done)
+
+    def roots(q, bank, done):
+        inc(pe.matmul(bank[:, 0:1], T.shr[0:32, :], T.sm[0:32, MW * q + 64:MW * q + 65], True, True), done)
+
+    need(pe, "c_y", "s_id")
+    need(act, "c_u")
+    turn_ids(rank, "v_own")
+    need(pe, "c_shr", "s_sm")
+    roots(rank, T.pb1, "p_ro")
+
     xbank = [T.pb2, T.pb3, T.pb4, T.pb6]
+
+    def turn(u, a):
+        p = (lo64, hi64)[a]
+        for j in range(2):
+            call = pe.matmul(xbank[u][p, j:128:2], T.xb[p, u + 4 * j, :, :], T.idb[p, p], True, True)
+        return call
+
     need(pe, "c_id")
+    if OPT["l8"]:
+        for h in range(8):
+            need(v, "ld_kid%d" % h)
+            p = (lo64, hi64)[h // 4]
+            if h < 7:
+                ts("x_lo" if h < 4 else "x_conv0", T.xb[p, :, h % 4, :], T.x[p, h % 4, :, :], -256.0, Op.add)
+            else:
+                for par in range(2):
+                    ts("x_conv%d" % par, T.xb[p, par:8:2, 3, :], T.x[p, 3, par:8:2, :], -256.0, Op.add)
+        need(pe, "x_lo")
+        for u in range(4):
+            turn(u, 0)
+    else:
+        for q4 in range(4):
+            need(v, "ld_kid%d" % q4)
+            for par in range(2):
+                ts("x_conv%d" % par, T.xb[:, par:8:2, q4, :], T.x[:, q4, par:8:2, :], -256.0, Op.add)
     for u in (0, 2, 1, 3):
         need(pe, "x_conv%d" % (u % 2))
-        for j in range(2):
-            for a in range(2):
-                p = slice(64 * a, 64 * a + 64)
-                inc(pe.matmul(xbank[u][p, j:128:2], T.xb[p, u + 4 * j, :, :], T.idb[p, p], True, True), "p_x%d" % u)
-    for u in (0, 2, 1, 3):
-        queue = (act, v)[u % 2]
+        if not OPT["l8"]:
+            turn(u, 0)
+        inc(turn(u, 1), "p_x%d" % u)
+    need(v, "p_ro")
+    ts("o_ls", T.rown[:, 0:1], T.pb1[:, 0:1], 256.0, Op.add)
+    need(v, "c_u", "c_id")
+    ts("c_w", T.cu[:, :], T.u[:, 3:4], C, Op.mult)
+    ts("c_w", T.cap[:, :], T.u[:, 2:3], NONE, Op.mult, -NONE, Op.add)
+    ts("c_hz", T.hz[:, :], T.gi[:, :], 16.0, Op.mult, 15.0, Op.add)
+    ts("c_h", T.hf[:, :], T.pq[:, :], 512.0, Op.mult, T.hq[:, :], Op.add)
+    inc(v.tensor_copy(T.sha[:, 0:127], T.idb[:, 1:128]), "z_sh")
+    for u, queue in ((0, act), (2, v), (1, act), (3, v)):
         need(queue, "p_x%d" % u)
         land, bank = T.w[:, cw + u:cw + M:4], xbank[u][:, 0:128]
-        inc(act.activation(land, bank, Act.Copy) if u % 2 == 0 else v.tensor_copy(land, bank), "w_own")
-    need(v, "w_own", "o_ls")
-    inc(v.tensor_copy(T.r[:, r0 + 64:r0 + 80], T.w[:, cw:cw + M].indirect(T.rown[:, 0:1])), "r_tmp")
-    need(v, "r_tmp")
-    ts("o_l2", T.lown[:, 0:4], T.r[:, r0 + 64 + o:r0 + 68 + o], 256.0, Op.add)
-    need(v, "o_l2")
-    inc(v.tensor_copy(T.r[:, r0:r0 + 64], T.w[:, cw:cw + M].indirect(T.lown[:, 0:4])), "r_own")
-    need(g, "r_tmp", "r_own")
-    spread(T.r[:, r0:r0 + R], T.r[:, r0:r0 + R], "r_arr", "r_out")
+        inc(act.activation(land, bank, Act.Copy) if queue is act else v.tensor_copy(land, bank), "w_own")
     need(g, "w_own")
-    spread(T.w[:, cw:cw + M], T.w[:, cw:cw + M], "w_arr", "w_out")
+    send(T.w[:, cw:cw + M], T.w[:, cw:cw + M], (twin, far_e, "w_twin"), (near, near_e, "w_near"))
 
+    wo, vo = T.w[:, cw:cw + M], T.v[:, cw:cw + M]
+    need(act, "o_ls", "v_own")
+    inc(act.activation(T.rid[:, :], vo.indirect(T.rown[:, 0:1]), Act.Copy), "a_rid")
     need(v, "ld_lett")
     inc(v.tensor_copy(T.lx[:, 0:48], T.li[:, 0:48]), "l_x")
-    need(act, "l_x", "c_u")
-    inc(act.activation(T.e[:, 32:S], T.u[:, 0:16].indirect(T.lx[:, 2:48]), Act.Copy), "e_main")
     ts("l_a", T.lq[:, :], T.li[:, 0:48], 12, Op.bitwise_and)
+    need(v, "w_own", "o_ls")
+    ts("o_l2", T.lown[:, :], wo.indirect(T.rown[:, 0:1]), 256.0, Op.add)
     ts("l_a", T.ln[:, :], T.li[:, 0:48], 16.0, Op.mult)
-    inc(v.tensor_copy(T.sha[:, 0:127], T.idb[:, 1:128]), "z_sh")
-    need(v, "l_a")
-    ts("l_b", T.lp[:, :], T.lq[:, :], 4.0, Op.mult)
-    ts("b_base", T.base[:, :], T.lq[:, :], 128.0, Op.mult, 256.0, Op.add)
-    need(v, "z_sh")
-    inc(v.memset(T.sha[:, 15:128:16], 0.0), "c_sh")
-    need(v, "l_b")
-    inc(v.tensor_tensor(T.lm[:, :], T.ln[:, :], T.lp[:, :], Op.add), "l_c")
     inc(v.tensor_copy(T.lf[:, :], T.li[:, 0:4]), "l_h")
-    need(v, "l_c")
-    inc(v.tensor_tensor(T.ls[:, 0:24], T.lm[:, 0:24], T.li[:, 1:25], Op.add), "l_e")
-    inc(v.memset(T.rl[:, :], 0), "z_rl")
-    need(v, "l_e")
-    inc(v.tensor_copy(T.letl[:, 0:24], T.ls[:, 0:24]), "l_l")
-    need(v, "c_grp", "z_sel", "z_sel2", "z_ones")
-    for h in range(8):
-        ts("c_sel", T.sel[:, 16 * h:2048:129], T.ones[:, 0:16], T.grp[:, h:h + 1], Op.mult)
-    ts("c_bc", T.basec[:, :], T.oi[:, :], 512.0, Op.mult, 1024.0, Op.add)
+    need(v, "c_h", "z_sh")
+    inc(v.memset(T.sha[:, 15:128:16], 0.0), "c_sh")
+    need(v, "o_l2")
+    inc(v.tensor_copy(T.r[:, r0:r0 + R], wo.indirect(T.lown[:, 0:4])), "r_own")
+    need(g, "r_own")
+    send(T.r[:, r0:r0 + R], T.r[:, r0:r0 + R], (other, far_e, "r_arr"), (near, near_e, "r_arr"))
+    need(act, "o_l2")
+    inc(act.activation(T.gb[:, :], vo.indirect(T.lown[:, 0:4]), Act.Copy), "a_gb")
+    need(v, "a_rid", "c_w")
+    ts("g_c", T.first[:, :], T.rid[:, 0:4], T.mul[:, :], Op.mult, T.u[:, 2:3], Op.subtract)
+    ts("c_sh", T.shb[0:32, :], T.rowi[0:32, 0:128], T.hf[0:32, :], Op.is_equal)
+    need(v, "a_gb", "g_c")
+    ts("g_m", T.ma[:, :], T.gb[:, :], 0.0, Op.max, T.cap[:, :], Op.min)
+    for f in range(4):
+        ts("g_m", T.mt[:, 16 * f:16 * f + 16], T.gb[:, 16 * f:16 * f + 16], 0.0, Op.is_lt, T.first[:, f:f + 1], Op.mult)
+    need(v, "l_a", "c_hz")
+    ts("b_base", T.base[:, :], T.lq[:, :], M / 4, Op.mult, 256.0, Op.add)
+    ts("c_wk", T.wk[:, :], T.rowi[:, 2:6], T.cu[:, :], Op.mult, T.mul[:, :], Op.add)
+    need(v, "g_m")
+    inc(v.tensor_tensor(T.d[:, r0:r0 + R], T.ma[:, :], T.mt[:, :], Op.add), "d_own")
+    ways = {"f": (far, far_e, "d_far"), "n": (near, near_e, "d_near")}
+    for c in OPT["order"].split():
+        if c == "on":
+            need(g, "w_twin")
+            send(T.w[:, M * qt:M * qt + M], T.w[:, M * qt:M * qt + M], (near, {"all": all_e, "n": near_e}[OPT["fe"]], "w_on"))
+        else:
+            need(g, "d_own")
+            send(T.d[:, r0:r0 + R], T.d[:, r0:r0 + R], *[ways[x] for x in c])
 
-    cn = MW * ((rank + 1) % n)
-    vb = [T.pb0, T.pb1, T.pb5, T.pb7]
-    need(pe, "c_y", "s_id")
-    for j in range(n):
-        q = (rank + j) % n
-        if j == 1:
-            need(pe, "c_sh", "l_h", "w_own", "s_sm", "sm_arr")
-            pe.matmul(T.pb2[:, 0:4], T.sha[:, :], T.lf[:, :], True, False)
-            inc(pe.matmul(T.pb2[:, 0:4], T.shb[0:8, :], T.sm[0:8, cn + 8:cn + 12], False, True), "p_halo")
-        for b in range(8):
-            inc(pe.matmul(vb[j][:, 64 * b:64 * b + 64], T.y[:, 128 * b:128 * b + 128], T.sm[:, MW * q + 16:MW * q + 80],
-                          True, True), "p_v%d" % j)
-        if j < n - 1:
-            need(act, "p_v%d" % j)
-            inc(act.activation(T.v[:, M * q:M * q + M], vb[j][:, :], Act.Copy), "v_in")
+    need(act, "l_x")
+    inc(act.activation(T.e[:, 32:S], T.u[:, 0:16].indirect(T.lx[:, 2:48]), Act.Copy), "e_main")
+    need(v, "h_arr")
+    inc(v.tensor_copy(T.hb[0:32, :], T.hin[0:32, :]), "l_hb")
+    ts("c_sel", T.sel[:, :], T.rowi[:, :], T.hz[:, :], Op.is_equal)
+    need(v, "c_wk")
+    ts("c_wb", T.wb[:, :], T.u[:, 2:3], C, Op.mult, T.wk[:, 0:1], Op.add)
+    need(pe, "c_sh", "l_h", "w_own", "l_hb")
+    pe.matmul(T.pb2[:, 0:4], T.sha[:, :], T.lf[:, :], True, False)
+    inc(pe.matmul(T.pb2[:, 0:4], T.shb[0:32, :], T.hb[0:32, :], False, True), "p_halo")
+    need(v, "c_sel")
+    for k in (3, 4, 5):
+        ts("c_z", T["z%d" % k][:, :], T.sel[:, :], T.wk[:, k - 2:k - 1], Op.mult)
     need(v, "p_halo")
     inc(v.tensor_copy(T.li[:, 48:52], T.pb2[:, 0:4]), "l_hx")
     inc(v.tensor_copy(T.lx[:, 48:52], T.pb2[:, 0:4]), "l_hx")
-    need(v, "sm_arr", "s_sm")
-    inc(v.tensor_reduce(T.rootc[:, :], T.sm[:, 0:MW * n:MW], AxisListType.X, Op.add), "r_col")
-    need(v, "l_hx", "c_u")
-    inc(v.tensor_tensor(T.ls[:, 24:48], T.lm[:, 24:48], T.li[:, 25:49], Op.add), "l_e2")
-    inc(v.tensor_copy(T.e[:, S:S + 64], T.u[:, 0:16].indirect(T.lx[:, 48:52])), "e_halo")
-    need(v, "l_e2")
-    inc(v.tensor_copy(T.letl[:, 24:48], T.ls[:, 24:48]), "l_l2")
-    need(v, "r_col", "c_bc")
-    ts("r_all", T.rall[:, 0:1], T.rootc[:, :], T.basec[:, :], Op.add)
-    need(v, "p_v%d" % (n - 1))
-    inc(v.tensor_copy(T.v[:, M * q:M * q + M], vb[n - 1][:, :]), "v_in2")
+    need(v, "c_wb")
+    ts("c_z", T.z2[:, :], T.sel[:, :], T.wb[:, :], Op.mult)
+    need(v, "l_hx")
+    inc(v.tensor_tensor(T.ls[:, :], T.ln[:, :], T.li[:, 1:49], Op.add), "l_s")
+    need(act, "l_hx")
+    inc(act.activation(T.e[:, S:S + 64], T.u[:, 0:16].indirect(T.lx[:, 48:52]), Act.Copy), "e_halo")
+
+    need(pe, "sm_arr", "o_ls")
+    roots(qt, T.pb3, "p_rt")
+    for q in (qn, qt, qo):
+        turn_ids(q, "v_in")
+    need(v, "p_rt")
+    ts("t_ls", T.rtwin[:, 0:1], T.pb3[:, 0:1], 256.0, Op.add)
+    need(v, "l_s")
+    inc(v.tensor_copy(T.ld[:, :], T.ls[:, :]), "l_d")
+    wt = T.w[:, M * qt:M * qt + M]
+    need(v, "w_twin", "t_ls")
+    ts("t_l2", T.ltwin[:, :], wt.indirect(T.rtwin[:, 0:1]), 256.0, Op.add)
+    need(v, "t_l2")
+    inc(v.tensor_copy(T.r[:, R * qt:R * qt + R], wt.indirect(T.ltwin[:, 0:4])), "t_own")
 
     win, win2 = T.w[:, 0:4 * M], T.v[:, 0:4 * M]
     lbank = {"a": T.pb2, "b": T.pb3}
-    zb = {1: T.pb0, 2: T.pb1, 3: T.pb5, 4: T.pb7}
+    zb = {2: T.pb0, 3: T.pb1}
+    z4 = {"a": T.pb5, "b": T.pb7}
     z5 = {"a": T.pb4, "b": T.pb6}
     part = {"a": 0, "b": 1}
 
     def step(k, f):
         h = part[f]
-        src = T.r[:, 0:4 * R].indirect(T.letl[:, 24 * h:24 * h + 24]) if k == 2 else \
+        src = T.r[:, 0:4 * R].indirect(T.ld[:, 24 * h:24 * h + 24]) if k == 2 else \
             win.indirect(T["list%d" % k][:, 24 * h:24 * h + 24])
         inc(v.tensor_tensor(T["m%d" % k][:, H * h:H * h + H], src, T.e[:, 16 * k + H * h:16 * k + H * h + H], Op.mult),
             "v_m%d%s" % (k, f))
@@ -231,111 +299,123 @@ def rank_program(g, core, T, topo):
         pe.matmul(out, T.idb[:, :], T.base[:, 24 * h:24 * h + 24], True, False)
         need(pe, "v_m%d%s" % (k, f))
         for i in range(16):
-            call = pe.matmul(out, T.sel[:, 128 * i:128 * i + 128], T["m%d" % k][:, H * h + i:H * h + H:16], False, i == 15)
+            call = pe.matmul(out, T.sel[:, 15 - i:143 - i], T["m%d" % k][:, H * h + i:H * h + H:16], False, i == 15)
         inc(call, "p_list%d%s" % (k + 1, f))
+        for j, key in ((2, "i12"), (3, "i3")):
+            if OPT[key] == "%d%s" % (k, f):
+                ids(j, "a_id%d" % j)
 
-    def take(k, f):
+    def take(k, f, between=None):
         h = part[f]
         need(v, "p_list%d%s" % (k, f))
         inc(v.tensor_copy(T["list%d" % k][:, 24 * h:24 * h + 24], lbank[f][:, 0:24]), "v_list%d%s" % (k, f))
+        if between:
+            between()
         need(v, "v_list%d%s" % (k, f))
 
-    def add_far(k, z):
-        pe.matmul(z, T.far[0:k, :], T.ones[0:k, 0:z.shape[1]], True, False)
-
-    def sums(k, z, col, s, last):
-        for b in range(4):
-            i = 4 * b + s
-            call = pe.matmul(z[0:32, col:col + 48], T.sel[:, 128 * i + s:128 * i + 128:4], T["a%d" % k][:, i:S:16],
-                             False, last and b == 3)
+    def sums(z, k, a, wide):
+        for s in range(4):
+            for b in range(4):
+                i = 4 * b + s
+                call = pe.matmul(z[0:32, wide * s:wide * s + wide], T["z%d" % k][:, 15 - i + s:143 - i:4], a(i), b == 0, b == 3)
         return call
 
     def ids(k, *waits):
+        need(pe, "c_z", "v_in", *waits)
+        inc(sums(zb[k], k, lambda i: T["a%d" % k][:, i:S:16], 48), "p_z%d" % k)
+
+    def ids_half(k, f, z, *waits):
         need(pe, *waits)
-        for s in range(4):
-            call = sums(k, zb[k], 48 * s, s, s == 3)
-        inc(call, "p_z%d" % k)
+        inc(sums(z, k, lambda i: T["a%d" % k][:, H * part[f] + i:H * part[f] + H:16], 24), "p_z%d%s" % (k, f))
 
-    def keep(k):
-        need(v, "p_z%d" % k, "d%d" % (k - 1))
-        inc(v.tensor_tensor(T.best[0:32, :], zb[k][0:32, 0:192], T.best[0:32, :], Op.max), "d%d" % k)
+    def read_ids(k, f, done):
+        h = part[f]
+        need(act, "v_list%d%s" % (k, f))
+        inc(act.activation(T["a%d" % k][:, H * h:H * h + H], win2.indirect(T["list%d" % k][:, 24 * h:24 * h + 24]), Act.Copy), done)
 
-    need(act, "v_in", "v_in2", "r_all")
-    inc(act.activation(T.rid[:, :], win2.indirect(T.rall[:, 0:1]), Act.Copy), "a_rid")
-    need(act, "a_rid")
-    inc(act.activation(T.a1[:, :], T.rid[:, 0:16].indirect(T.lx[:, 0:48]), Act.Copy), "a_id1")
-    need(v, "r_arr", "l_l", "e_main")
+    def half(t, f):
+        return t[0:32, :, 24 * part[f]:24 * part[f] + 24]
+
+    need(v, "r_arr", "r_own", "t_own", "l_d", "e_main")
     step(2, "a")
-    need(v, "l_l2", "e_halo")
+    need(v, "e_halo")
     step(2, "b")
-    need(v, "z_rl")
-    for q in range(n):
-        ts("r_l", T.rl[:, 5 * q:5 * q + 4], T.r[:, R * q + 64 + 4 * q:R * q + 68 + 4 * q], 256.0 + M * q, Op.add)
-    need(act, "r_l")
-    inc(act.activation(T.ridb[:, :], win2.indirect(T.rl[:, 0:20]), Act.Copy), "a_ridb")
-    need(act, "a_ridb", "l_l", "l_l2")
-    inc(act.activation(T.a2[:, :], T.ridb[:, 0:4 * R].indirect(T.letl[:, 0:48]), Act.Copy), "a_id2")
-    need(pe, "b_base", "c_sel", "l_hx", "z_ones")
-    for f in "ab":
-        add_far(5, z5[f][0:32, 0:96])
+    need(act, "d_near", "d_far", "d_own", "l_d")
+    inc(act.activation(T.a2[:, :], T.d[:, 0:4 * R].indirect(T.ld[:, 0:48]), Act.Copy), "a_id2")
+    need(pe, "b_base", "c_sel", "l_hx", "t_ls")
     wrap(2, "a")
     wrap(2, "b")
-    need(pe, "v_in", "v_in2")
-    for k in (1, 2, 3, 4):
-        add_far(k, zb[k][0:32, 0:192])
-    ids(1, "a_id1")
-    take(3, "a")
-    take(3, "b")
-    need(act, "v_list3a", "v_list3b")
-    inc(act.activation(T.a3[:, :], win2.indirect(T.list3[:, 0:48]), Act.Copy), "a_id3")
-    need(v, "w_arr")
+    take(3, "a", lambda: need(v, "w_near", "w_on"))
     step(3, "a")
+    take(3, "b")
     step(3, "b")
+    need(act, "v_own", "v_in")
+    for f in "ab":
+        read_ids(3, f, "a_id3")
     wrap(3, "a")
     wrap(3, "b")
-    ids(2, "a_id2")
     for f in "ab":
         take(4, f)
         step(4, f)
-        h = part[f]
-        need(act, "v_list4" + f)
-        inc(act.activation(T.a4[:, H * h:H * h + H], win2.indirect(T.list4[:, 24 * h:24 * h + 24]), Act.Copy), "a_id4" + f)
+        read_ids(4, f, "a_id4" + f)
+        if f == "a":
+            need(act, "p_z2")
+            inc(act.activation(T.best[0:32, :, :], zb[2][0:32, 0:192], Act.Relu), "d2")
         wrap(4, f)
-    ids(3, "a_id3")
-    ids(4, "a_id4a", "a_id4b")
-    need(act, "p_z1")
-    inc(act.activation(T.best[0:32, :], zb[1][0:32, 0:192], Act.Relu), "d1")
-    need(v, "v_in", "v_in2")
-    take(5, "a")
-    inc(v.tensor_copy(T.a5[:, 0:H], win2.indirect(T.list5[:, 0:24])), "v_id5a")
+        if f == "b" and not OPT["i4"]:
+            ids_half(4, "a", z4["a"], "a_id4a")
+        if f == "b" or OPT["i4"]:
+            ids_half(4, f, z4[f], "a_id4" + f)
+
+    top = {f: T.pb2[0:32, 96 * part[f]:96 * part[f] + 96] for f in "ab"}
+
+    def keep(f):
+        need(v, "p_z4" + f, "d3")
+        inc(v.tensor_tensor(half(T.best, f), z4[f][0:32, 0:96], half(T.best, f), Op.max), "d4" + f)
+
+    def longest(f):
+        need(v, "p_z5" + f, "d4" + f)
+        inc(v.tensor_tensor(top[f], z5[f][0:32, 0:96], half(T.best, f), Op.max), "d5" + f)
+
+    def length(f):
+        need(v, "d5" + f)
+        ts("rr_ok" + f, half(T.rr, f), top[f], BIG, Op.add, -BIG, Op.add)
+        need(act, "rr_ok" + f)
+        inc(act.activation(half(T.yl, f), half(T.rr, f), Act.Copy, scale=1.0 / C), "yl_ok" + f)
+
+    def rest(f):
+        need(v, "rr_ok" + f)
+        inc(v.tensor_tensor(half(T.yi, f), top[f], half(T.rr, f), Op.subtract), "yi_ok" + f)
+
+    def third():
+        need(v, "p_z3", "d2")
+        inc(v.tensor_tensor(T.best[0:32, :, :], zb[3][0:32, 0:192], T.best[0:32, :, :], Op.max), "d3")
+
+    need(v, "v_own", "v_in")
+    take(5, "a", third)
+    if OPT["a5"] == "act":
+        read_ids(5, "a", "v_id5a")
+    else:
+        need(act, "v_list5a")
+        inc(act.activation(T.a5[:, 0:256], win2.indirect(T.list5[:, 0:16]), Act.Copy), "v_id5a")
+        inc(v.tensor_copy(T.a5[:, 256:H], win2.indirect(T.list5[:, 16:24])), "v_id5a")
+    if OPT["i4"]:
+        keep("a")
     take(5, "b")
     inc(v.tensor_copy(T.a5[:, H:H + 192], win2.indirect(T.list5[:, 24:36])), "v_id5b")
     need(act, "v_list5b")
     inc(act.activation(T.a5[:, H + 192:S], win2.indirect(T.list5[:, 36:48]), Act.Copy), "a_id5")
-    for k in (2, 3, 4):
-        keep(k)
-    need(pe, "v_id5a", "v_id5b", "a_id5")
-    for f in "ab":
-        for j in range(2):
-            call = sums(5, z5[f], 48 * j, 2 * part[f] + j, j == 1)
-        inc(call, "p_z5" + f)
-
-    half = {f: slice(96 * part[f], 96 * part[f] + 96) for f in "ab"}
-    for f in "ab":
-        need(v, "p_z5" + f, "d4")
-        inc(v.tensor_tensor(T.pb2[0:32, half[f]], z5[f][0:32, 0:96], T.best[0:32, half[f]], Op.max), "d5" + f)
-    for f in "ab":
-        need(v, "d5" + f)
-        ts("rr_ok" + f, T.rr[0:32, half[f]], T.pb2[0:32, half[f]], BIG, Op.add, -BIG, Op.add)
-    for f in "ab":
-        need(v, "rr_ok" + f)
-        inc(v.tensor_tensor(T.yi[0:32, half[f]], T.pb2[0:32, half[f]], T.rr[0:32, half[f]], Op.subtract), "yi_ok" + f)
-        need(act, "rr_ok" + f)
-        inc(act.activation(T.yl[0:32, half[f]], T.rr[0:32, half[f]], Act.Copy, scale=1.0 / C), "yl_ok" + f)
+    ids_half(5, "a", z5["a"], "v_id5a")
+    ids_half(5, "b", z5["b"], "v_id5b", "a_id5")
+    if not OPT["i4"]:
+        keep("a")
+    keep("b")
+    for c in OPT["end"].split():
+        {"L": longest, "n": length, "r": rest}[c[0]](c[1])
     need(act, "yl_oka", "yl_okb")
-    inc(act.dma_start(T.ylen[:, :], T.yl[0:32, :]), "st_len", 16)
+    inc(act.dma_start(T.ylen[:, :], T.yl[0:32, :, :]), "st_len", 16)
     need(sp, "yi_oka", "yi_okb")
-    inc(sp.dma_start(T.yid[:, :], T.yi[0:32, :]), "st_id", 16)
+    inc(sp.dma_start(T.yid[:, :], T.yi[0:32, :, :]), "st_id", 16)
     need(act, "st_len")
     need(sp, "st_id")
-    need(g, "sm_out", "w_out", "r_out")
+    need(g, "sent")

from concourse.bass import DstId, RemoteDMATransfer
from concourse.mybir import AluOpType as Op, ActivationFunctionType as Act

S, M = 768, 512
H = S // 2
MW = 72
R = 64
C = 131072.0
BIG = 1.5 * 2.0 ** 40
NONE = -2.0 ** 24
OPT = dict(i12="3a", i3="3b", i4=True, end="La na Lb ra nb rb", order="fn on", fe="all", l8=False, a5="act")
SCRATCH = {"x": ("sbuf", [128, 4, 8, 16], "int32"), "xb": ("sbuf", [128, 8, 4, 16], "bfloat16")}
for _t, _s in (("int32", "li52 hm4 hin4 rw1 ti64 tb64 pi1 ci1 gi1 pq1 lq48 ln48 ls48 rowi144 yv64"),
               ("float32", "tz64 pf1 cf1 hf1 hq1 hs1 hz1 cap1 wk4 wb1 first4 ma64 mt64"),
               ("uint16", "rown2 rtwin2 lown16 ltwin16 ld48 lx52"),
               ("bfloat16", "mul1 cu1 lf4 hb4 sm288 w2048 v2048 e832 sel144 y1024 idb128 sha128 shb128 shr128 u16 base48 r256 "
                            "d256 rid16 gb64")):
    for _n in _s.split():
        _b = _n.rstrip("0123456789")
        SCRATCH[_b] = ("sbuf", [128, int(_n[len(_b):])], _t)
for _n in ("best", "rr", "yl", "yi"):
    SCRATCH[_n] = ("sbuf", [128, 4, 48], "float32")
for _k in (3, 4, 5):
    SCRATCH["list%d" % _k] = ("sbuf", [128, 48], "uint16")
for _k in range(2, 6):
    SCRATCH["a%d" % _k] = ("sbuf", [128, S], "bfloat16")
    SCRATCH["z%d" % _k] = ("sbuf", [128, 144], "bfloat16")
for _k in (2, 3, 4):
    SCRATCH["m%d" % _k] = ("sbuf", [128, S], "bfloat16")
for _k in range(8):
    SCRATCH["pb%d" % _k] = ("psum", [128, 512], "float32")
SEMAPHORES = ("ld_lett ld_halo ld_root ld_tid ld_tid2 ld_kid0 ld_kid1 ld_kid2 ld_kid3 ld_kid4 ld_kid5 ld_kid6 ld_kid7 h_arr sm_arr "
              "w_twin w_near w_on r_arr d_near d_far sent st_id st_len iota iota2 z_y z_hm z_sm z_sh c_a c_b c_id c_u c_h c_h0 "
              "c_hs c_shr c_sh c_hz c_y c_sel c_w c_wk c_wb c_z s_th s_id s_sm l_x l_a l_s l_d b_base p_halo p_ro p_rt l_h l_hb "
              "l_hx o_ls o_l2 w_own r_own t_ls t_l2 t_own e_main e_halo a_rid a_gb g_c g_m d_own a_id2 a_id3 x_lo x_conv0 x_conv1 "
              "p_x0 p_x1 p_x2 p_x3 p_v0 p_v1 p_v2 p_v3 v_own v_in p_z2 p_z3 d2 d3 a_id5").split()
for _f in "ab":
    SEMAPHORES += [_n + _f for _n in ("v_m2", "v_m3", "v_m4", "p_list3", "p_list4", "p_list5", "v_list3", "v_list4", "v_list5",
                                      "a_id4", "p_z4", "d4", "v_id5", "p_z5", "d5", "rr_ok", "yi_ok", "yl_ok")]


def rank_program(g, core, T, topo):
    rank = T.rank_of(core)
    if rank is None:
        return
    n = len(T.cores)
    v, pe, act, sp = g.vector, g.tensor, g.scalar, g.sync
    count = {}

    def inc(call, name, by=1):
        call.then_inc(T.sem[name], by)
        count[name] = count.get(name, 0) + by

    def need(queue, *names):
        for name in names:
            queue.wait_ge(T.sem[name], count[name])

    def ts(name, out, in0, s1, op0, s2=None, op1=None):
        inc(v.tensor_scalar(out, in0, s1, None, op0) if op1 is None else v.tensor_scalar(out, in0, s1, s2, op0, op1), name)

    near = [d for d in T.cores if d != core and d in topo.cores_of(core)]
    far = [d for d in T.cores if d != core and d not in topo.cores_of(core)]
    twin = [d for d in far if topo.die(d) == topo.die(core)]
    other = [d for d in far if d not in twin]
    far_e = [e for e in range(16) if all(e in topo.engines(core, d) for d in far)]
    all_e = [e for e in range(16) if all(e in topo.engines(core, d) for d in near)]
    near_e = [e for e in all_e if e not in far_e]
    qt, qn, qo = (T.rank_of(d[0]) for d in (twin, near, other))
    before, after = T.cores[(rank - 1) % n], T.cores[(rank + 1) % n]

    def send(piece, land, *ways):
        tr = []
        for ds, es, arr in ways:
            ids = []
            for d in ds:
                rid, pid = topo.addr(d, core)
                ids.append(DstId(rid=rid, pnc=pid))
            tr.append(RemoteDMATransfer(dst_ids=ids, dma_engine_mask=sum(1 << e for e in es),
                                        remote_sem=T.sem[arr], srcs=[piece], dsts=[land for _ in ds]))
            count["sent"] = count.get("sent", 0) + len(es)
            count[arr] = count.get(arr, 0) + len(es) * len(ds)
        g.remote_dma_fused(tr, local_sem=T.sem["sent"])

    c0, cw, r0, o = MW * rank, M * rank, R * rank, 4 * rank
    lo64, hi64 = slice(0, 64), slice(64, 128)
    inc(sp.dma_start(T.hm[0:32, :], T.lett[:, 0:16]), "ld_halo", 16)
    inc(act.dma_start(T.ti[lo64, :], T.tid[:, :]), "ld_tid", 16)
    inc(sp.dma_start(T.ti[hi64, :], T.tid[:, :]), "ld_tid2", 16)
    inc(act.dma_start(T.rw[0:32, :], T.kid[:, 16 + o:20 + o]), "ld_root", 16)
    if OPT["l8"]:
        for h in range(8):
            inc((sp, act)[h % 2].dma_start(T.x[(lo64, hi64)[h // 4], h % 4, :, :], T.kid[h:h + 1, :]), "ld_kid%d" % h, 16)
    else:
        for q4 in range(4):
            inc((sp, act)[q4 % 2].dma_start(T.x[:, q4, :, :], T.kid[q4:8:4, :]), "ld_kid%d" % q4, 16)
    inc(sp.dma_start(T.li[:, 0:48], T.lett[:, :]), "ld_lett", 16)

    inc(v.memset(T.hm[32:64, :], 0), "z_hm")
    inc(v.memset(T.hm[hi64, :], 0), "z_hm")
    inc(g.iota(T.pi[:, :], [[0, 1]], 0, 1), "iota")
    inc(g.iota(T.rowi[:, :], [[1, 144]], 0, 0), "iota")
    inc(g.iota(T.yv[:, :], [[1, 8], [8, 8]], 0, 0), "iota2")
    need(g, "z_hm", "ld_halo")
    send(T.hm[:, :], T.hin[:, :], ([before], topo.engines(core, before), "h_arr"))
    count["h_arr"] = len(topo.engines(after, core))

    inc(v.memset(T.sm[:, c0 + 64:c0 + MW], 0.0), "z_sm")
    inc(v.memset(T.y[:, :], 0.0), "z_y")
    need(v, "iota")
    ts("c_a", T.ci[:, :], T.pi[:, :], 15, Op.bitwise_and)
    inc(v.tensor_copy(T.pf[:, :], T.pi[:, :]), "c_a")
    ts("c_h0", T.pq[:, :], T.pi[:, :], 3, Op.bitwise_and)
    ts("c_h0", T.hq[:, :], T.pi[:, :], 4.0, Op.mult, 15.0, Op.add)
    ts("c_h0", T.gi[:, :], T.pi[:, :], 4, Op.arith_shift_right)
    need(v, "c_a")
    ts("c_id", T.idb[:, :], T.rowi[:, 0:128], T.pf[:, :], Op.is_equal)
    inc(v.tensor_copy(T.cf[:, :], T.ci[:, :]), "c_b")
    ts("c_b", T.mul[:, :], T.ci[:, :], 2.0, Op.is_lt)
    need(v, "iota2", "z_y")
    ts("c_y", T.y[:, 0:1024:16], T.yv[:, :], T.pf[:, :], Op.is_equal)
    for row in (1, 2):
        ts("c_y", T.y[:, row:1024:16], T.yv[:, :], 64.0, Op.add, T.pf[:, :], Op.is_equal)
    need(v, "c_b", "c_h0")
    ts("c_u", T.u[:, :], T.rowi[:, 0:16], T.cf[:, :], Op.is_equal)
    ts("c_hs", T.hs[:, :], T.pq[:, :], -3.0, Op.mult, T.hq[:, :], Op.add)

    need(v, "ld_tid")
    ts("s_th", T.tb[lo64, :], T.ti[lo64, :], 65280, Op.bitwise_and)
    need(v, "ld_tid2")
    ts("s_th", T.tb[hi64, :], T.ti[hi64, :], 255, Op.bitwise_and)
    ts("s_th", T.tz[:, :], T.ti[:, :], 0.0, Op.is_equal, NONE, Op.mult)
    need(v, "ld_root", "z_sm", "c_hs")
    ts("s_sm", T.sm[0:32, c0 + 64:c0 + 65], T.rw[0:32, :], -256.0, Op.add)
    ts("c_shr", T.shr[0:32, :], T.rowi[0:32, 0:128], 15.0, Op.add, T.hs[0:32, :], Op.is_equal)
    need(v, "s_th")
    inc(v.tensor_tensor(T.sm[:, c0:c0 + 64], T.tb[:, :], T.tz[:, :], Op.add), "s_id")
    need(g, "s_id", "s_sm")
    send(T.sm[:, c0:c0 + MW], T.sm[:, c0:c0 + MW], (far, far_e, "sm_arr"), (near, near_e, "sm_arr"))

    vb = {rank: T.pb0, qt: T.pb1, qn: T.pb5, qo: T.pb7}

    def turn_ids(q, done):
        for b in range(8):
            call = pe.matmul(vb[q][:, 64 * b:64 * b + 64], T.y[:, 128 * b:128 * b + 128], T.sm[:, MW * q:MW * q + 64], True, True)
        inc(call, "p_v%d" % q)
        need(act, "p_v%d" % q)
        inc(act.activation(T.v[:, M * q:M * q + M], vb[q][:, :], Act.Identity, bias=T.u[:, 3:4]), done)

    def roots(q, bank, done):
        inc(pe.matmul(bank[:, 0:1], T.shr[0:32, :], T.sm[0:32, MW * q + 64:MW * q + 65], True, True), done)

    need(pe, "c_y", "s_id")
    need(act, "c_u")
    turn_ids(rank, "v_own")
    need(pe, "c_shr", "s_sm")
    roots(rank, T.pb1, "p_ro")

    xbank = [T.pb2, T.pb3, T.pb4, T.pb6]

    def turn(u, a):
        p = (lo64, hi64)[a]
        for j in range(2):
            call = pe.matmul(xbank[u][p, j:128:2], T.xb[p, u + 4 * j, :, :], T.idb[p, p], True, True)
        return call

    need(pe, "c_id")
    if OPT["l8"]:
        for h in range(8):
            need(v, "ld_kid%d" % h)
            p = (lo64, hi64)[h // 4]
            if h < 7:
                ts("x_lo" if h < 4 else "x_conv0", T.xb[p, :, h % 4, :], T.x[p, h % 4, :, :], -256.0, Op.add)
            else:
                for par in range(2):
                    ts("x_conv%d" % par, T.xb[p, par:8:2, 3, :], T.x[p, 3, par:8:2, :], -256.0, Op.add)
        need(pe, "x_lo")
        for u in range(4):
            turn(u, 0)
    else:
        for q4 in range(4):
            need(v, "ld_kid%d" % q4)
            for par in range(2):
                ts("x_conv%d" % par, T.xb[:, par:8:2, q4, :], T.x[:, q4, par:8:2, :], -256.0, Op.add)
    for u in (0, 2, 1, 3):
        need(pe, "x_conv%d" % (u % 2))
        if not OPT["l8"]:
            turn(u, 0)
        inc(turn(u, 1), "p_x%d" % u)
    need(v, "p_ro")
    ts("o_ls", T.rown[:, 0:1], T.pb1[:, 0:1], 256.0, Op.add)
    need(v, "c_u", "c_id")
    ts("c_w", T.cu[:, :], T.u[:, 3:4], C, Op.mult)
    ts("c_w", T.cap[:, :], T.u[:, 2:3], NONE, Op.mult, -NONE, Op.add)
    ts("c_hz", T.hz[:, :], T.gi[:, :], 16.0, Op.mult, 15.0, Op.add)
    ts("c_h", T.hf[:, :], T.pq[:, :], 512.0, Op.mult, T.hq[:, :], Op.add)
    inc(v.tensor_copy(T.sha[:, 0:127], T.idb[:, 1:128]), "z_sh")
    for u, queue in ((0, act), (2, v), (1, act), (3, v)):
        need(queue, "p_x%d" % u)
        land, bank = T.w[:, cw + u:cw + M:4], xbank[u][:, 0:128]
        inc(act.activation(land, bank, Act.Copy) if queue is act else v.tensor_copy(land, bank), "w_own")
    need(g, "w_own")
    send(T.w[:, cw:cw + M], T.w[:, cw:cw + M], (twin, far_e, "w_twin"), (near, near_e, "w_near"))

    wo, vo = T.w[:, cw:cw + M], T.v[:, cw:cw + M]
    need(act, "o_ls", "v_own")
    inc(act.activation(T.rid[:, :], vo.indirect(T.rown[:, 0:1]), Act.Copy), "a_rid")
    need(v, "ld_lett")
    inc(v.tensor_copy(T.lx[:, 0:48], T.li[:, 0:48]), "l_x")
    ts("l_a", T.lq[:, :], T.li[:, 0:48], 12, Op.bitwise_and)
    need(v, "w_own", "o_ls")
    ts("o_l2", T.lown[:, :], wo.indirect(T.rown[:, 0:1]), 256.0, Op.add)
    ts("l_a", T.ln[:, :], T.li[:, 0:48], 16.0, Op.mult)
    inc(v.tensor_copy(T.lf[:, :], T.li[:, 0:4]), "l_h")
    need(v, "c_h", "z_sh")
    inc(v.memset(T.sha[:, 15:128:16], 0.0), "c_sh")
    need(v, "o_l2")
    inc(v.tensor_copy(T.r[:, r0:r0 + R], wo.indirect(T.lown[:, 0:4])), "r_own")
    need(g, "r_own")
    send(T.r[:, r0:r0 + R], T.r[:, r0:r0 + R], (other, far_e, "r_arr"), (near, near_e, "r_arr"))
    need(act, "o_l2")
    inc(act.activation(T.gb[:, :], vo.indirect(T.lown[:, 0:4]), Act.Copy), "a_gb")
    need(v, "a_rid", "c_w")
    ts("g_c", T.first[:, :], T.rid[:, 0:4], T.mul[:, :], Op.mult, T.u[:, 2:3], Op.subtract)
    ts("c_sh", T.shb[0:32, :], T.rowi[0:32, 0:128], T.hf[0:32, :], Op.is_equal)
    need(v, "a_gb", "g_c")
    ts("g_m", T.ma[:, :], T.gb[:, :], 0.0, Op.max, T.cap[:, :], Op.min)
    for f in range(4):
        ts("g_m", T.mt[:, 16 * f:16 * f + 16], T.gb[:, 16 * f:16 * f + 16], 0.0, Op.is_lt, T.first[:, f:f + 1], Op.mult)
    need(v, "l_a", "c_hz")
    ts("b_base", T.base[:, :], T.lq[:, :], M / 4, Op.mult, 256.0, Op.add)
    ts("c_wk", T.wk[:, :], T.rowi[:, 2:6], T.cu[:, :], Op.mult, T.mul[:, :], Op.add)
    need(v, "g_m")
    inc(v.tensor_tensor(T.d[:, r0:r0 + R], T.ma[:, :], T.mt[:, :], Op.add), "d_own")
    ways = {"f": (far, far_e, "d_far"), "n": (near, near_e, "d_near")}
    for c in OPT["order"].split():
        if c == "on":
            need(g, "w_twin")
            send(T.w[:, M * qt:M * qt + M], T.w[:, M * qt:M * qt + M], (near, {"all": all_e, "n": near_e}[OPT["fe"]], "w_on"))
        else:
            need(g, "d_own")
            send(T.d[:, r0:r0 + R], T.d[:, r0:r0 + R], *[ways[x] for x in c])

    need(act, "l_x")
    inc(act.activation(T.e[:, 32:S], T.u[:, 0:16].indirect(T.lx[:, 2:48]), Act.Copy), "e_main")
    need(v, "h_arr")
    inc(v.tensor_copy(T.hb[0:32, :], T.hin[0:32, :]), "l_hb")
    ts("c_sel", T.sel[:, :], T.rowi[:, :], T.hz[:, :], Op.is_equal)
    need(v, "c_wk")
    ts("c_wb", T.wb[:, :], T.u[:, 2:3], C, Op.mult, T.wk[:, 0:1], Op.add)
    need(pe, "c_sh", "l_h", "w_own", "l_hb")
    pe.matmul(T.pb2[:, 0:4], T.sha[:, :], T.lf[:, :], True, False)
    inc(pe.matmul(T.pb2[:, 0:4], T.shb[0:32, :], T.hb[0:32, :], False, True), "p_halo")
    need(v, "c_sel")
    for k in (3, 4, 5):
        ts("c_z", T["z%d" % k][:, :], T.sel[:, :], T.wk[:, k - 2:k - 1], Op.mult)
    need(v, "p_halo")
    inc(v.tensor_copy(T.li[:, 48:52], T.pb2[:, 0:4]), "l_hx")
    inc(v.tensor_copy(T.lx[:, 48:52], T.pb2[:, 0:4]), "l_hx")
    need(v, "c_wb")
    ts("c_z", T.z2[:, :], T.sel[:, :], T.wb[:, :], Op.mult)
    need(v, "l_hx")
    inc(v.tensor_tensor(T.ls[:, :], T.ln[:, :], T.li[:, 1:49], Op.add), "l_s")
    need(act, "l_hx")
    inc(act.activation(T.e[:, S:S + 64], T.u[:, 0:16].indirect(T.lx[:, 48:52]), Act.Copy), "e_halo")

    need(pe, "sm_arr", "o_ls")
    roots(qt, T.pb3, "p_rt")
    for q in (qn, qt, qo):
        turn_ids(q, "v_in")
    need(v, "p_rt")
    ts("t_ls", T.rtwin[:, 0:1], T.pb3[:, 0:1], 256.0, Op.add)
    need(v, "l_s")
    inc(v.tensor_copy(T.ld[:, :], T.ls[:, :]), "l_d")
    wt = T.w[:, M * qt:M * qt + M]
    need(v, "w_twin", "t_ls")
    ts("t_l2", T.ltwin[:, :], wt.indirect(T.rtwin[:, 0:1]), 256.0, Op.add)
    need(v, "t_l2")
    inc(v.tensor_copy(T.r[:, R * qt:R * qt + R], wt.indirect(T.ltwin[:, 0:4])), "t_own")

    win, win2 = T.w[:, 0:4 * M], T.v[:, 0:4 * M]
    lbank = {"a": T.pb2, "b": T.pb3}
    zb = {2: T.pb0, 3: T.pb1}
    z4 = {"a": T.pb5, "b": T.pb7}
    z5 = {"a": T.pb4, "b": T.pb6}
    part = {"a": 0, "b": 1}

    def step(k, f):
        h = part[f]
        src = T.r[:, 0:4 * R].indirect(T.ld[:, 24 * h:24 * h + 24]) if k == 2 else \
            win.indirect(T["list%d" % k][:, 24 * h:24 * h + 24])
        inc(v.tensor_tensor(T["m%d" % k][:, H * h:H * h + H], src, T.e[:, 16 * k + H * h:16 * k + H * h + H], Op.mult),
            "v_m%d%s" % (k, f))

    def wrap(k, f):
        h = part[f]
        if k > 2:
            need(pe, "v_list%d%s" % (k, f))
        out = lbank[f][:, 0:24]
        pe.matmul(out, T.idb[:, :], T.base[:, 24 * h:24 * h + 24], True, False)
        need(pe, "v_m%d%s" % (k, f))
        for i in range(16):
            call = pe.matmul(out, T.sel[:, 15 - i:143 - i], T["m%d" % k][:, H * h + i:H * h + H:16], False, i == 15)
        inc(call, "p_list%d%s" % (k + 1, f))
        for j, key in ((2, "i12"), (3, "i3")):
            if OPT[key] == "%d%s" % (k, f):
                ids(j, "a_id%d" % j)

    def take(k, f, between=None):
        h = part[f]
        need(v, "p_list%d%s" % (k, f))
        inc(v.tensor_copy(T["list%d" % k][:, 24 * h:24 * h + 24], lbank[f][:, 0:24]), "v_list%d%s" % (k, f))
        if between:
            between()
        need(v, "v_list%d%s" % (k, f))

    def sums(z, k, a, wide):
        for s in range(4):
            for b in range(4):
                i = 4 * b + s
                call = pe.matmul(z[0:32, wide * s:wide * s + wide], T["z%d" % k][:, 15 - i + s:143 - i:4], a(i), b == 0, b == 3)
        return call

    def ids(k, *waits):
        need(pe, "c_z", "v_in", *waits)
        inc(sums(zb[k], k, lambda i: T["a%d" % k][:, i:S:16], 48), "p_z%d" % k)

    def ids_half(k, f, z, *waits):
        need(pe, *waits)
        inc(sums(z, k, lambda i: T["a%d" % k][:, H * part[f] + i:H * part[f] + H:16], 24), "p_z%d%s" % (k, f))

    def read_ids(k, f, done):
        h = part[f]
        need(act, "v_list%d%s" % (k, f))
        inc(act.activation(T["a%d" % k][:, H * h:H * h + H], win2.indirect(T["list%d" % k][:, 24 * h:24 * h + 24]), Act.Copy), done)

    def half(t, f):
        return t[0:32, :, 24 * part[f]:24 * part[f] + 24]

    need(v, "r_arr", "r_own", "t_own", "l_d", "e_main")
    step(2, "a")
    need(v, "e_halo")
    step(2, "b")
    need(act, "d_near", "d_far", "d_own", "l_d")
    inc(act.activation(T.a2[:, :], T.d[:, 0:4 * R].indirect(T.ld[:, 0:48]), Act.Copy), "a_id2")
    need(pe, "b_base", "c_sel", "l_hx", "t_ls")
    wrap(2, "a")
    wrap(2, "b")
    take(3, "a", lambda: need(v, "w_near", "w_on"))
    step(3, "a")
    take(3, "b")
    step(3, "b")
    need(act, "v_own", "v_in")
    for f in "ab":
        read_ids(3, f, "a_id3")
    wrap(3, "a")
    wrap(3, "b")
    for f in "ab":
        take(4, f)
        step(4, f)
        read_ids(4, f, "a_id4" + f)
        if f == "a":
            need(act, "p_z2")
            inc(act.activation(T.best[0:32, :, :], zb[2][0:32, 0:192], Act.Relu), "d2")
        wrap(4, f)
        if f == "b" and not OPT["i4"]:
            ids_half(4, "a", z4["a"], "a_id4a")
        if f == "b" or OPT["i4"]:
            ids_half(4, f, z4[f], "a_id4" + f)

    top = {f: T.pb2[0:32, 96 * part[f]:96 * part[f] + 96] for f in "ab"}

    def keep(f):
        need(v, "p_z4" + f, "d3")
        inc(v.tensor_tensor(half(T.best, f), z4[f][0:32, 0:96], half(T.best, f), Op.max), "d4" + f)

    def longest(f):
        need(v, "p_z5" + f, "d4" + f)
        inc(v.tensor_tensor(top[f], z5[f][0:32, 0:96], half(T.best, f), Op.max), "d5" + f)

    def length(f):
        need(v, "d5" + f)
        ts("rr_ok" + f, half(T.rr, f), top[f], BIG, Op.add, -BIG, Op.add)
        need(act, "rr_ok" + f)
        inc(act.activation(half(T.yl, f), half(T.rr, f), Act.Copy, scale=1.0 / C), "yl_ok" + f)

    def rest(f):
        need(v, "rr_ok" + f)
        inc(v.tensor_tensor(half(T.yi, f), top[f], half(T.rr, f), Op.subtract), "yi_ok" + f)

    def third():
        need(v, "p_z3", "d2")
        inc(v.tensor_tensor(T.best[0:32, :, :], zb[3][0:32, 0:192], T.best[0:32, :, :], Op.max), "d3")

    need(v, "v_own", "v_in")
    take(5, "a", third)
    if OPT["a5"] == "act":
        read_ids(5, "a", "v_id5a")
    else:
        need(act, "v_list5a")
        inc(act.activation(T.a5[:, 0:256], win2.indirect(T.list5[:, 0:16]), Act.Copy), "v_id5a")
        inc(v.tensor_copy(T.a5[:, 256:H], win2.indirect(T.list5[:, 16:24])), "v_id5a")
    if OPT["i4"]:
        keep("a")
    take(5, "b")
    inc(v.tensor_copy(T.a5[:, H:H + 192], win2.indirect(T.list5[:, 24:36])), "v_id5b")
    need(act, "v_list5b")
    inc(act.activation(T.a5[:, H + 192:S], win2.indirect(T.list5[:, 36:48]), Act.Copy), "a_id5")
    ids_half(5, "a", z5["a"], "v_id5a")
    ids_half(5, "b", z5["b"], "v_id5b", "a_id5")
    if not OPT["i4"]:
        keep("a")
    keep("b")
    for c in OPT["end"].split():
        {"L": longest, "n": length, "r": rest}[c[0]](c[1])
    need(act, "yl_oka", "yl_okb")
    inc(act.dma_start(T.ylen[:, :], T.yl[0:32, :, :]), "st_len", 16)
    need(sp, "yi_oka", "yi_okb")
    inc(sp.dma_start(T.yid[:, :], T.yi[0:32, :, :]), "st_id", 16)
    need(act, "st_len")
    need(sp, "st_id")
    need(g, "sent")
